import numpy as np, ml_dtypes
CORES = [3,7,11,15,131,135,139,143]
N = 8
import mx_ref
BF = ml_dtypes.bfloat16
def tile(rs):
    return np.stack(rs, axis=2).reshape(128, -1).astype(BF)
def pick(q, e):
    c = np.concatenate([q[0].reshape(128, -1, 4), np.zeros((128, 1, 4), np.uint8)], axis=1); s = np.concatenate([q[1], np.ones((16, 1), np.uint8)], axis=1)
    return (np.ascontiguousarray(c[:, e].reshape(128, -1)), np.ascontiguousarray(s[:, e]))
def join(*qs):
    return (np.concatenate([q[0] for q in qs], axis=1), np.concatenate([q[1] for q in qs], axis=1))
def put(q, e, v):
    c, s = q[0].reshape(128, -1, 4).copy(), q[1].copy(); c[:, e] = v[0].reshape(128, -1, 4); s[:, e] = v[1]
    return (c.reshape(128, -1), s)
def pk(c, s):
    return (np.ascontiguousarray(c), mx_ref.live(s))
def emit(q):
    return q[0], q[1]
def packed(v, rng):
    q = [mx_ref.quantize(np.ascontiguousarray(v[r])) for r in range(N)]
    return np.stack([a for a, b in q]), np.stack([mx_ref.plane(b, rng) for a, b in q])
def values_of_codes():
    e, c = np.zeros((128, 128, 4), np.float32), np.zeros((128, 2, 4), np.uint8)
    e[np.arange(128), np.arange(128), 0] = 1
    c[:127, :, 0] = np.arange(256).reshape(2, 128).T[:127]
    return mx_ref.matmul(mx_ref.quantize(e.reshape(128, 512).astype(BF)), (c.reshape(128, 8), np.full((16, 2), 127, np.uint8))).T.reshape(-1).astype(np.float64)
CODE_VALUE, SCALE_VALUE = values_of_codes(), 2.0 ** (np.arange(256) - 127.0)
def decode(q):
    return (CODE_VALUE[q[0]].reshape(16, 8, -1, 4) * SCALE_VALUE[q[1]][:, None, :, None] + 0.0).reshape(128, -1).astype(np.float32)
def f(rng, *shape):
    return mx_ref.flush((rng.standard_normal(shape, dtype=np.float32) * np.exp2(rng.integers(-2, 3, shape[:-1] + (1,)))).astype(BF))
def wide(rng, *shape, cols=0):
    v = rng.standard_normal(shape, dtype=np.float32) * np.exp2(rng.integers(-12, 13, shape)).astype(np.float32)
    if cols: v *= np.repeat(np.exp2(rng.integers(-cols, cols + 1, shape[:-2] + (1, shape[-1] // 4))) * (rng.random(shape[:-2] + (1, shape[-1] // 4)) > 0.0625), 4, axis=-1).astype(np.float32)
    return mx_ref.flush(v.astype(BF))
C, H = 224, 112
MASK = [1, 2, 4]
def numbers_of(rng):
    return {"x": np.array(f(rng, N, 128, 4 * C)), "u": np.array(f(rng, N, 128, 512)), "v": np.array(f(rng, N, 128, 512))}
def layers(rng, still=[]):
    w = np.array(mx_ref.flush((np.clip(f(rng, N, 128, 2048).astype(np.float32), -4, 4) * np.float32(0.125)).astype(BF))).reshape(N, 8, 16, 4, 8, 16, 4)
    for i in still: w[:, :, :, :, :, i] = 0
    return w
def weights(rng, w):
    c, p = packed(np.ascontiguousarray(w).reshape(N, 128, 2048), rng)
    return {"wc": c, "ws": p}
def setup_inputs(rng):
    return {**numbers_of(rng), **weights(rng, layers(rng))}
def setup_inputs_ties(rng):
    d = numbers_of(rng)
    o = rng.permutation(N)
    x = d["x"].reshape(N, 8, 16, C, 4)
    k = rng.integers(0, 3, (N, 8, C)) - 4 * (o % 2)[:, None, None]
    k[o == 2] = np.arange(8)[:, None]
    x[:, :, 0] = 0
    x[:, :, 0, :, 0] = k.astype(np.float32).astype(BF)
    z = 1 + 32 * rng.permutation(C // 32)[np.arange(C) // 32] + rng.permutation(32)[np.arange(C) % 32]
    z = 4 * z[None, :] + ((np.arange(8) + int(rng.choice([2, 4, 6]))) % 8 // 2)[:, None]
    for r in range(N):
        if o[r] == 3: x[r, :, 0] = (-((z[:, :, None] >> (3 * np.arange(4))) & 7)).astype(np.float32).astype(BF)
    n = (N, 8, 8, C, 4)
    a = (129 + 2 * rng.integers(0, 64, n)) * np.exp2(-7.0 - rng.integers(8, 15, n)) * (rng.integers(0, 2, n) * 2.0 - 1.0)
    a[:, :, 0, :, 0] = 1.96875
    a = a * np.exp2(1.0 * rng.integers(-2, 3, (N, 8, 1, C, 1)))
    x[:, :, 8:] = a.astype(np.float32).astype(BF)
    u = d["u"].reshape(N, 128, 128, 4)
    u[:, :, ::16] = 0
    for r in range(N):
        for h in range(0, 128, 16):
            u[r, h, h, 0] = 0.0 if o[r] == 0 else -1.0 if o[r] == 1 else 1.0
            if o[r] == 3: u[r, h, h] = np.exp2(3.0 * np.arange(4)).astype(np.float32).astype(BF)
    return {"x": x.reshape(N, 128, 4 * C), "u": u.reshape(N, 128, 512), "v": d["v"], **weights(rng, layers(rng, [0] + [*range(8, 16)]))}
def setup_inputs_near(rng):
    d = numbers_of(rng)
    x = d["x"].astype(np.float32).reshape(N, 8, 16, C, 4)
    x[:, :, 0] = 0
    x[:, :, 8:] = 0
    u = d["u"].reshape(N, 128, 128, 4)
    u[:, :, ::16] = 0
    o = rng.permutation(N) % 4
    for r in range(N):
        s = rng.integers(0, 16, (8, C, 1))
        if o[r] < 3: x[r, :, 8] = ((s >> np.arange(4)) & 1) * np.exp2(np.arange(4) - 23.0)
        if o[r] < 2:
            x[r, :, 0, :, 0] = rng.integers(0, 2, (8, C)) * 2.0 - 1.0
            x[r, :, 11, :, 0] = 2.0 ** -10
        if o[r] == 2:
            e = rng.permutation(8)
            x[r, e[0], 0, :, 0] = 1.0
            x[r, e[1], 0, :, 0] = -1.0
        if o[r] == 3:
            x[r, :4, 10, :, 0] = rng.choice([1.0, 2.0], (4, C)) * 2.0 ** -30
            x[r, 4:, 10, :, 0] = rng.choice([1.125, 2.0], (4, C)) * 2.0 ** -30
            t = rng.permutation(C)[:C // 4]
            z = rng.integers(0, 2, (8, C // 4)) * 0.25
            c = np.where(np.arange(8) < 4, 1.0, 1.125)[:, None]
            x[r][:, 10, t, 0] = (c + z) * 2.0 ** -30
            x[r][:, 12, t, 0] = (c - z - 2.125) * 2.0 ** -30
        k = 1.0 if o[r] == 0 else 2.0 ** -30
        for h in range(0, 128, 16):
            u[r, h, h, 0] = 1.0 if o[r] == 2 else k
            u[r, h + 8, h] = k
            u[r, h + 11, h, 0] = k
            u[r, h + 10, h, 0] = k if o[r] < 3 else k * 1.25 if h < 64 else k * 1.125
            u[r, h + 12, h, 0] = 0.0 if o[r] < 3 else k * 1.125 if h < 64 else k * 1.25
    return {"x": x.reshape(N, 128, 4 * C).astype(BF), "u": u.reshape(N, 128, 512), "v": d["v"], **weights(rng, layers(rng, [0] + [*range(8, 16)]))}
def setup_inputs_huge(rng):
    d = numbers_of(rng)
    o = rng.permutation(N) % 2
    c = rng.integers(0, 2, (N, 1, 1, C, 1)) * 2.0 - 1.0
    c[o == 0] = -1.0
    x = (0.6 + 0.08 * rng.random((N, 8, 16, C, 4))) * 2.0 ** 30 * c
    a = 2.0 ** 30 * (1.0 - 0.1 * rng.random((N, 128, 8, 4)))
    a[o == 1] *= rng.choice([-1.0, 1.0], (N // 2, 1, 8, 1))
    u = d["u"].reshape(N, 128, 128, 4)
    u[:, :, ::16] = a.astype(np.float32).astype(BF)
    w = rng.integers(1, 3, (N, 8, 16, 4, 8, 16, 4)) * 2.0 ** -9 * rng.choice([-1.0, 1.0], (N, 1, 1, 4, 8, 16, 1))
    return {"x": x.astype(np.float32).reshape(N, 128, 4 * C).astype(BF), "u": u.reshape(N, 128, 512), "v": d["v"], **weights(rng, w.astype(np.float32).astype(BF))}
def setup_inputs_ends(rng):
    d = numbers_of(rng)
    o = rng.permutation(N) % 4
    most, least = 255.0 * 2.0 ** 22, 2.0 ** -30
    x = np.full((N, 8, C), least)
    u = d["u"].reshape(N, 8, 16, 128, 4)
    v = rng.choice([-1.0, 1.0], (N, 128, 512))
    for r in range(N):
        a = np.ones((8, 16, 8, 4)) * (2.0 ** -30 if o[r] == 2 else 2.0 ** 30)
        if o[r] == 0:
            x[r] = -most
            for g in rng.permutation(8)[:4]: a[:, :, g] *= rng.choice([0.5, 1.0], (8, 16, 4))
        else: a *= rng.choice([-1.0, 1.0], (8, 1, 8, 1))
        if o[r] == 1: x[r] = most * rng.choice([-1.0, 1.0], (1, C))
        if o[r] == 3: x[r] = np.where(rng.random((8, C)) < 0.5, least, most * rng.choice([-1.0, 1.0], (8, C)))
        u[r][:, :, ::16] = a.astype(np.float32).astype(BF)
        v[r] *= 2.0 ** 30 if o[r] % 2 == 0 else 2.0 ** -30
    x = x[:, :, None, :, None] * np.ones((1, 1, 16, 1, 4))
    w = rng.choice([-1.0, 1.0], (N, 8, 16, 1, 8, 2, 1, 4)) * np.full((1, 1, 1, 4, 1, 1, 8, 1), least)
    return {"x": x.astype(np.float32).reshape(N, 128, 4 * C).astype(BF), "u": u.reshape(N, 128, 512), "v": v.astype(np.float32).astype(BF), **weights(rng, w.astype(np.float32).astype(BF))}
def setup_inputs_spread(rng):
    d = setup_inputs(rng)
    d["x"] = wide(rng, N, 128, 4 * C, cols=2)
    return d
def check_inputs(d):
    b = []
    for k in ("x", "u", "v"):
        a = np.abs(d[k].astype(np.float32))
        if not (np.isfinite(a).all() and ((a == 0) | (a >= 2.0 ** -30) & (a <= 2.0 ** 30)).all()): b.append("a value of " + k)
    none, least, most = [emit(mx_ref.quantize(np.full((128, 16), k, np.float32).astype(BF)))[1][0, 0] for k in (0.0, 2.0 ** -30, 2.0 ** 30)]
    top = 0.0
    for r in range(N):
        if ((d["wc"][r] == 0x7F) | (d["wc"][r] == 0xFF)).any(): b.append("wc: a code that is no number")
        s = mx_ref.live(d["ws"][r])
        if ((s != none) & ((s < least) | (s > most))).any(): b.append("ws: a scale out of range")
        top = max(top, float(np.abs(decode(pk(d["wc"][r], d["ws"][r]))).max()))
    if not float(np.abs(d["x"].astype(np.float32)).max()) * (1.0 + 32.0 * top) * (1.0 + 32.0 * top) * (1.0 + 32.0 * top) <= 2.0 ** 30: b.append("x and W: too large together")
    return b
def reference(x, u, v, wc, ws):
    qu = [mx_ref.quantize(u[r]) for r in range(N)]
    lay = [pk(wc[r], ws[r]) for r in range(N)]
    now = [x[r] for r in range(N)]
    place = np.zeros((N, 8 * C), np.int64)
    for m in MASK:
        seats, made = [], []
        for r in range(N):
            q = mx_ref.quantize(now[r])
            own = decode(q).astype(BF).reshape(8, 16, C, 4)
            s = mx_ref.matmul(qu[r], q)[::16] + np.float32(0.0)
            o = np.argsort(-s.reshape(-1), kind="stable")
            place[r, o] = np.arange(8 * C)
            t = own[o // C, :, o % C].reshape(C, 8, 16, 4).transpose(1, 2, 0, 3)
            seats.append(mx_ref.quantize(np.ascontiguousarray(t).reshape(128, 4 * C)))
        for r in range(N):
            q = join(pick(seats[r ^ m], np.arange(H)), pick(seats[r], np.arange(H, C)))
            a = decode(q)
            t = tile([np.maximum(mx_ref.matmul(pick(lay[r], np.arange(128 * b, 128 * b + 128)), q), np.float32(0.0)) * np.float32(0.03125) + a[:, b::4] for b in range(4)])
            n = place[r].reshape(8, C)
            home = t.reshape(8, 16, C, 4)[n % 8, :, n // 8]
            made.append(np.ascontiguousarray(home.transpose(0, 2, 1, 3)).reshape(128, 4 * C))
        now = made
    y, pl = np.zeros((N, 128, C), np.float32), np.zeros((N, 8, C), np.float32)
    oc, osc = np.zeros((N, 128, 4 * C), np.uint8), np.zeros((N, 16, C), np.uint8)
    for r in range(N):
        q = mx_ref.quantize(now[r])
        y[r] = mx_ref.matmul(mx_ref.quantize(v[r]), q)
        pl[r] = place[r].reshape(8, C)
        oc[r], osc[r] = emit(q)
    return {"y": y, "pl": pl, "oc": oc, "osc": osc}

@@ -1,0 +1,387 @@
+from concourse.bass import DstId, RemoteDMATransfer
+from concourse.mybir import dt, AluOpType as ALU, ActivationFunctionType as ACT
+
+C, H = 224, 112
+MASK = [1, 2, 4]
+SLOT = 1024
+F8, U8, BF, FP, I32, U16 = "float8_e4m3fn_x4", "uint8", "bfloat16", "float32", "int32", "uint16"
+
+SCRATCH = {}
+
+
+def _sb(name, n, d):
+    SCRATCH[name] = ("sbuf", [128, n], d)
+
+
+def _mx(code, plane, n):
+    _sb(code, n, F8)
+    _sb(plane, n, U8)
+
+
+for _n, _w, _d in [
+        ("XT", 4 * C, BF), ("UT", 512, BF), ("VIN", 512, BF), ("ET", 2048, BF), ("OT", 960, BF), ("WRT", 512, BF),
+        ("SB", 8 * C, FP), ("SJ", 16, FP), ("R", 16, FP), ("J0", 8 * C, BF), ("J1", 8 * C, BF),
+        ("WINF", 8 * SLOT, BF), ("WINT", 8 * SLOT, BF), ("WSP", 8 * C, FP), ("MG", 112, FP), ("M1", 56, FP), ("M2", 28, FP), ("M3", 14, FP),
+        ("X1", 16, I32), ("X2", 16, I32), ("LF", 64, U16), ("LH", 64, U16), ("SO", 16, U16),
+        ("RI", 16, I32), ("D4", 64, I32), ("DB", 64, BF), ("RM", 512, BF), ("RB", 176, FP), ("RW", 16, FP),
+        ("TM", C, FP), ("T1", 112, FP), ("T2", 56, FP), ("T3", 28, FP), ("T4", 14, FP), ("L1", 14, FP), ("LB", 32, FP), ("TR", 32, FP),
+        ("I3", 48, I32), ("WP", 48, FP), ("PM", 48, FP), ("PA", 16, FP), ("PA2", 16, FP),
+        ("HB", 16, I32), ("HC", 16, I32), ("HD", 16, I32), ("HO", 16, I32),
+        ("TL", 512, BF), ("TU", 512, BF), ("RL", 512, FP), ("Y", C, FP),
+        ("KI", C, I32), ("KJ", C, I32), ("DM", C, FP), ("P8", 8, I32), ("P9", 8, I32), ("MK", 8, FP), ("PI", 8, I32), ("GI", 8, I32), ("EI", 8, I32),
+        ("HADJ", 8, FP), ("G1024", 8, FP), ("IDV0", C, FP), ("IDV", C, FP), ("NM0", 14, FP), ("G208", 8, FP), ("NM", 14, FP),
+        ("CA", 8, FP), ("CB", 8, FP), ("CC", 8, FP), ("CD", 8, FP), ("CE", 8, FP), ("CGO", 8, U16), ("UI", 64, I32), ("UO", 64, U16), ("JM", 8, FP), ("JB", 8, FP)]:
+    _sb(_n, _w, _d)
+for _n, _w in [("X", C), ("U", 128), ("UB", 1024), ("V", 128), ("W", 512), ("E", 512), ("O", 240), ("WR", 128), ("RQ", 128), ("L", 128), ("B0", 240), ("B1", 240), ("B2", 240)]:
+    _mx(_n + "c", _n + "p", _w)
+for _a in range(4):
+    _sb("VT%d" % _a, 4 * 448 * (_a + 1), BF)
+    _mx("K%dc" % _a, "K%dp" % _a, 448 * (_a + 1))
+for _n in range(8):
+    SCRATCH["PB%d" % _n] = ("psum", [128, 512], FP)
+
+SEMAPHORES = ["cv", "cs", "ct", "cg"] + ["d%d" % k for k in range(60)] + ["ls%d" % k for k in range(3)] + ["ar%d" % k for k in range(3)]
+
+
+def rank_program(g, core, T, topo):
+    rank = T.rank_of(core)
+    if rank is None:
+        return
+    Q = {"v": g.vector, "s": g.scalar, "t": g.tensor, "g": g, "y": g.sync}
+    SEM = {"v": "cv", "s": "cs", "t": "ct", "g": "cg"}
+    total = {}
+    known = {q: {} for q in Q}
+    snap = {}
+    hist = {}
+    nd = [0]
+
+    def learn(q, sem, c):
+        k = known[q]
+        if k.get(sem, 0) >= c:
+            return
+        Q[q].wait_ge(T.sem[sem], c)
+        k[sem] = c
+        for s2, c2 in snap.get((sem, c), {}).items():
+            if k.get(s2, 0) < c2:
+                k[s2] = c2
+
+    def spread(regs):
+        out = []
+        for r in regs:
+            out.append((r[0], 0, 512, None) if r[0][:2] == "PB" else (r + (None,))[:4])
+        return out
+
+    def before(q, kind, reads, writes):
+        need = {}
+        for w, regs in ((False, reads), (True, writes)):
+            for (b, lo, hi, ph) in regs:
+                for e in hist.get(b, []):
+                    elo, ehi, eph, ew, eq, ek, es, ec = e
+                    if elo >= hi or lo >= ehi or (ph is not None and eph is not None and ph != eph):
+                        continue
+                    if b[:2] == "PB":
+                        if eq == q:
+                            continue
+                    elif not (w or ew):
+                        continue
+                    need[es] = max(need.get(es, 0), ec)
+        for s, c in sorted(need.items(), key=lambda x: -len(snap.get(x, {}))):
+            learn(q, s, c)
+
+    def after(q, kind, reads, writes, sem, c):
+        for w, regs in ((False, reads), (True, writes)):
+            for (b, lo, hi, ph) in regs:
+                old = hist.setdefault(b, [])
+                keep = []
+                for e in old:
+                    inside = e[0] >= lo and e[1] <= hi and (ph is None or ph == e[2])
+                    if inside and ((w and b[:2] != "PB") or (e[4] == q and e[5] == "c" and kind == "c" and (e[3] == w or b[:2] == "PB"))):
+                        if not (e[6] == sem and e[7] == c):
+                            continue
+                    keep.append(e)
+                keep.append((lo, hi, ph, w, q, kind, sem, c))
+                hist[b] = keep
+
+    def op(q, fn, reads, writes):
+        reads, writes = spread(reads), spread(writes)
+        before(q, "c", reads, writes)
+        sem = SEM[q]
+        fn(Q[q]).then_inc(T.sem[sem], 1)
+        total[sem] = total.get(sem, 0) + 1
+        snap[(sem, total[sem])] = dict(known[q])
+        after(q, "c", reads, writes, sem, total[sem])
+
+    def dmas(items):
+        sem = "d%d" % nd[0]
+        nd[0] += 1
+        sn = {}
+        items = [(q, o, i, spread(r), spread(w)) for q, o, i, r, w in items]
+        for q, o, i, r, w in items:
+            before(q, "d", r, w)
+            Q[q].dma_start(o, i).then_inc(T.sem[sem], 16)
+            for s2, c2 in known[q].items():
+                sn[s2] = max(sn.get(s2, 0), c2)
+        total[sem] = 16 * len(items)
+        snap[(sem, total[sem])] = sn
+        for q, o, i, r, w in items:
+            after(q, "d", r, w, sem, total[sem])
+
+    def quant(code, plane, a, n, src, s0):
+        op("v", lambda e: e.quantize_mx(T[code][:, a:a + n], T[plane][:, a:a + n], T[src][:, s0:s0 + 4 * n]),
+           [(src, s0, s0 + 4 * n)], [(code, a, a + n), (plane, a, a + n)])
+
+    def mm(bank, L, l0, R, r0, n, start=True, stop=True):
+        op("t", lambda e: e.matmul_mx(T[bank][:, 0:n], T[L + "c"][:, l0:l0 + 128], T[L + "p"][:, l0:l0 + 128], T[R + "c"][:, r0:r0 + n], T[R + "p"][:, r0:r0 + n], start, stop),
+           [(L + "c", l0, l0 + 128), (L + "p", l0, l0 + 128), (R + "c", r0, r0 + n), (R + "p", r0, r0 + n)], [(bank, 0, 512)])
+
+    def ap(r):
+        return T[r[0]][:, r[1]:r[2]:r[3]] if len(r) > 3 else T[r[0]][:, r[1]:r[2]]
+
+    def rg(r):
+        return (r[0], r[1], r[2], r[1] % 4) if len(r) > 3 and r[3] == 4 else (r[0], r[1], r[2])
+
+    def ts(out, in0, s1, s2, o0, o1=None, q="v"):
+        rs = [rg(in0)] + [s for s in (s1, s2) if isinstance(s, tuple)]
+        a1 = ap(s1) if isinstance(s1, tuple) else s1
+        a2 = ap(s2) if isinstance(s2, tuple) else s2
+        if o1 is None:
+            op(q, lambda e: e.tensor_scalar(ap(out), ap(in0), a1, None, o0), rs, [rg(out)])
+        else:
+            op(q, lambda e: e.tensor_scalar(ap(out), ap(in0), a1, a2, o0, o1), rs, [rg(out)])
+
+    def tt(out, a, b, o):
+        op("v", lambda e: e.tensor_tensor(ap(out), ap(a), ap(b), o), [rg(a), rg(b)], [rg(out)])
+
+    def cp(out, a):
+        op("v", lambda e: e.tensor_copy(ap(out), ap(a)), [rg(a)], [rg(out)])
+
+    def acp(out, a):
+        op("s", lambda e: e.activation(ap(out), ap(a), ACT.Copy), [rg(a)], [rg(out)])
+
+    def ms(out, val):
+        op("v", lambda e: e.memset(ap(out), val), [], [rg(out)])
+
+    def iota(out, pattern, base, mult, flag=False):
+        if flag:
+            op("g", lambda e: e.iota(ap(out), pattern, base, mult, allow_small_or_imprecise_dtypes=True), [], [rg(out)])
+        else:
+            op("g", lambda e: e.iota(ap(out), pattern, base, mult), [], [rg(out)])
+
+    def gather(q, out, win, off):
+        src = ap(win).indirect(ap(off))
+        if q == "v":
+            op("v", lambda e: e.tensor_copy(ap(out), src), [rg(win), rg(off)], [rg(out)])
+        else:
+            op("s", lambda e: e.activation(ap(out), src, ACT.Copy), [rg(win), rg(off)], [rg(out)])
+
+    dmas([("y", T.XT[:], T.x[:], [], [("XT", 0, 4 * C)])])
+    dmas([("s", T.UT[:], T.u[:], [], [("UT", 0, 512)])])
+    dmas([("y", T.Wc[:].bitcast(dt.uint8), T.wc[:], [], [("Wc", 0, 512)]), ("y", T.Wp[:], T.ws[:], [], [("Wp", 0, 512)]),
+          ("y", T.VIN[:], T.v[:], [], [("VIN", 0, 512)])])
+
+    iota(("UI", 0, 64), [[16, 8], [0, 8]], 0, 0)
+    iota(("PI", 0, 8), [[0, 8]], 0, 1)
+    cp(("UO", 0, 64), ("UI", 0, 64))
+    ts(("JM", 0, 8), ("PI", 0, 8), 32, None, ALU.is_ge)
+    ts(("JB", 0, 8), ("JM", 0, 8), -1.0, 1e29, ALU.add, ALU.mult)
+    ms(("ET", 0, 2048), 1.0)
+    op("g", lambda e: e.affine_select(T.ET[:], T.ET[:], [[1, 4], [-1, 512]], ALU.is_equal, 0.0, 0, 4), [("ET", 0, 2048)], [("ET", 0, 2048)])
+    iota(("KI", 0, C), [[1, C]], 256, -1)
+    iota(("P8", 0, 8), [[-16, 8]], 0, 1)
+    iota(("IDV0", 0, C), [[4, C]], 0, 0, True)
+    iota(("NM0", 0, 14), [[16, 14]], 0, 1, True)
+    for A in (1, 3, 2, 0):
+        ms(("VT%d" % A, 4 * (448 * A + 128), 4 * 448 * (A + 1)), 0.0)
+    quant("Uc", "Up", 0, 128, "UT", 0)
+    op("s", lambda e: e.activation(T.UBp[:, 0:1024], T.Up[:, 0:128].indirect(T.UO[:, 0:64]), ACT.Copy),
+       [("Up", 0, 128), ("UO", 0, 64)], [("UBp", 0, 1024)])
+    op("v", lambda e: e.tensor_copy(T.UBc[:, 0:1024].bitcast(dt.uint32), T.Uc[:, 0:128].bitcast(dt.uint32).indirect(T.UO[:, 0:64])),
+       [("Uc", 0, 128), ("UO", 0, 64)], [("UBc", 0, 1024)])
+    quant("Xc", "Xp", 0, C, "XT", 0)
+    quant("Ec", "Ep", 0, 512, "ET", 0)
+
+    def more_constants():
+        ms(("OT", 0, 960), 0.0)
+        ms(("OT", 448, 512), 1.0)
+        quant("Oc", "Op", 0, 240, "OT", 0)
+        ts(("KJ", 0, C), ("KI", 0, C), 15, None, ALU.bitwise_and)
+        ts(("DM", 0, C), ("KJ", 0, C), 0, None, ALU.is_equal)
+        ms(("WRT", 0, 512), 0.0)
+        for d, w in enumerate((1.0, 16.0, 256.0)):
+            ts(("WRT", d, 512, 4), ("DM", 0, 128), w, None, ALU.mult)
+        quant("WRc", "WRp", 0, 128, "WRT", 0)
+        ts(("P9", 0, 8), ("P8", 0, 8), 4, None, ALU.arith_shift_right)
+        ts(("MK", 0, 8), ("P9", 0, 8), 0, None, ALU.is_equal)
+        ts(("GI", 0, 8), ("PI", 0, 8), 4, None, ALU.arith_shift_right)
+        ts(("EI", 0, 8), ("PI", 0, 8), 15, None, ALU.bitwise_and)
+        ts(("HADJ", 0, 8), ("GI", 0, 8), -1024.0, 8192.0, ALU.mult, ALU.add)
+        ts(("G1024", 0, 8), ("GI", 0, 8), 1024.0, None, ALU.mult)
+        ts(("G208", 0, 8), ("GI", 0, 8), 208.0, None, ALU.mult)
+        ts(("IDV", 0, C), ("IDV0", 0, C), ("G1024", 0, 1), None, ALU.add)
+        ts(("NM", 0, 14), ("NM0", 0, 14), ("G208", 0, 1), None, ALU.add)
+        ts(("CA", 0, 8), ("EI", 0, 8), 8, -95.0, ALU.is_ge, ALU.mult)
+        ts(("CB", 0, 8), ("EI", 0, 8), 16.0, None, ALU.mult)
+        ts(("CC", 0, 8), ("GI", 0, 8), 2.0, None, ALU.mult)
+        tt(("CD", 0, 8), ("CA", 0, 8), ("CB", 0, 8), ALU.add)
+        tt(("CE", 0, 8), ("CC", 0, 8), ("CD", 0, 8), ALU.add)
+        cp(("CGO", 0, 8), ("CE", 0, 8))
+        ms(("RB", 0, 176), 0.0)
+        ms(("D4", 0, 64), 0)
+        ms(("LB", 0, 32), 0.0)
+        ms(("I3", 0, 48), 0)
+        for k, w in enumerate((1.75, 222.25, -223.0)):
+            ms(("WP", 16 * k, 16 * k + 16), w)
+        for k in range(8):
+            ms(("WINF", SLOT * k + 896, SLOT * k + SLOT), 0.0)
+            ms(("WINT", SLOT * k + 896, SLOT * k + SLOT), 0.0)
+
+    def replicate(win, lo, hi, queues):
+        items = []
+        for k in range(1, 8):
+            o = SLOT * k
+            p = 128 - 16 * k
+            rd, wr = [(win, lo, hi)], [(win, o + lo, o + hi)]
+            items.append((queues[k % len(queues)], T[win][0:p, o + lo:o + hi], T[win][16 * k:128, lo:hi], rd, wr))
+            items.append((queues[(k + 1) % len(queues)], T[win][p:128, o + lo:o + hi], T[win][0:16 * k, lo:hi], rd, wr))
+        dmas(items)
+
+    partners = [T.cores[rank ^ m] for m in MASK]
+    lanes = [e for e in topo.engines(core, partners[0]) if all(e in topo.engines(core, p) for p in partners)]
+    emask = sum(1 << e for e in lanes)
+
+    for rnd in range(3):
+        B = "B%d" % rnd
+        last = rnd == 2
+        for half in range(2):
+            mm("PB%d" % (4 + half), "X", 96 * half, "U", 0, 128)
+        cp(("SJ", 0, 16, 2), ("PB4", 0, 128, 16))
+        ts(("SJ", 1, 16, 2), ("PB5", 0, 128, 16), ("JM", 0, 1), ("JB", 0, 1), ALU.mult, ALU.add)
+        for h in range(8):
+            mm("PB%d" % (h % 4), "UB", 128 * h, "X", 0, C)
+            (cp if h in (1, 3) else acp)(("SB", C * h, C * h + C), ("PB%d" % (h % 4), 0, C))
+        for b in range(4):
+            mm("PB%d" % b, "E", 128 * b, "X", 0, C)
+            acp(("WINF", b, 896, 4), ("PB%d" % b, 0, C))
+        replicate("WINF", 0, 896, "y")
+
+        first = [True]
+
+        def compare(a):
+            A, t, h, half = a // 4, a % 4, a // 2, a % 2
+            n = C * h + (C if half else 128)
+            i0, m = (C * h + 128, 96) if half else (C * h, 128)
+            vt = "VT%d" % A
+            ts((vt, t, 4 * n, 4), ("SB", 0, n), ("SJ", a, a + 1), None, ALU.is_lt)
+            d = (vt, 4 * i0 + t, 4 * n, 4)
+            op("g", lambda e: e.affine_select(ap(d), ap(d), [[-1, m]], ALU.is_gt, 0.0, -32 * half, 1), [rg(d)], [rg(d)])
+            j = "J%d" % (a % 2)
+            op("s", lambda e: e.activation(T[j][:, 0:n], T[vt][:, t:4 * n:4], ACT.Copy, accum_out=T.R[:, a:a + 1]),
+               [(vt, t, 4 * n, t)], [(j, 0, n), ("R", a, a + 1)])
+
+        def count(A, final):
+            for p in range(A + 1):
+                quant("K%dc" % A, "K%dp" % A, 448 * p, 448, "VT%d" % A, 1792 * p)
+                for h in (2 * p, 2 * p + 1):
+                    mm("PB6", "O", 112 - 16 * h, "K%d" % A, C * h, C, first[0], final and h == 2 * A + 1)
+                    first[0] = False
+
+        for a in (4, 5, 6, 7):
+            compare(a)
+        iota(("WSP", 0, 8 * C), [[0, 8 * C]], 0, 0, True)
+        for a in (12, 13):
+            compare(a)
+        if rnd == 0:
+            more_constants()
+        count(1, False)
+        for a in (14, 15, 8, 9):
+            compare(a)
+        count(3, False)
+        for a in (10, 11, 0, 1, 2, 3):
+            compare(a)
+        count(2, False)
+        count(0, True)
+        cp(("RI", 0, 16), ("R", 0, 16))
+        ts(("D4", 0, 64, 4), ("RI", 0, 16), 15, None, ALU.bitwise_and)
+        ts(("D4", 1, 64, 4), ("RI", 0, 16), 4, 15, ALU.logical_shift_right, ALU.bitwise_and)
+        ts(("D4", 2, 64, 4), ("RI", 0, 16), 8, None, ALU.logical_shift_right)
+        cp(("DB", 0, 64), ("D4", 0, 64))
+        for k in range(8):
+            o = ("RM", 64 * k, 64 * k + 64)
+            if k % 2:
+                op("s", lambda e: e.activation(ap(o), T.DB[:, 0:64], ACT.Copy, scale=T.MK[:, k:k + 1]), [("DB", 0, 64), ("MK", k, k + 1)], [rg(o)])
+            else:
+                ts(o, ("DB", 0, 64), ("MK", k, k + 1), None, ALU.mult)
+        quant("RQc", "RQp", 0, 128, "RM", 0)
+        mm("PB7", "WR", 0, "RQ", 0, 128)
+        acp(("RB", 0, 128), ("PB7", 0, 128))
+        tt(("TM", 0, C), ("PB6", 0, C), ("DM", 0, C), ALU.mult)
+        src = ("TM", C)
+        for nxt in ("T1", "T2", "T3", "T4"):
+            w = src[1]
+            tt((nxt, 0, w // 2), (src[0], 0, w, 2), (src[0], 1, w, 2), ALU.add)
+            src = (nxt, w // 2)
+        gather("v", ("RW", 0, 16), ("RB", 0, 176), ("CGO", 0, 1))
+        tt(("L1", 0, 14), ("NM", 0, 14), ("RW", 0, 14), ALU.subtract)
+        tt(("I3", 0, 14), ("L1", 0, 14), ("T4", 0, 14), ALU.add)
+        ts(("I3", 16, 30), ("I3", 0, 14), 7, None, ALU.bitwise_and)
+        ts(("I3", 32, 46), ("I3", 0, 14), 7, None, ALU.logical_shift_right)
+        tt(("PM", 0, 48), ("I3", 0, 48), ("WP", 0, 48), ALU.mult)
+        tt(("PA", 0, 16), ("PM", 0, 16), ("PM", 16, 32), ALU.add)
+        tt(("PA2", 0, 16), ("PA", 0, 16), ("PM", 32, 48), ALU.add)
+        cp(("SO", 0, 16), ("PA2", 0, 16))
+        op("v", lambda e: e.tensor_copy(T.WSP[:, 0:8 * C].indirect(T.SO[:, 0:14]), T.IDV[:, 0:C]),
+           [("SO", 0, 14), ("IDV", 0, C)], [("WSP", 0, 8 * C)])
+        dmas([("ys"[h % 2], T.MG[:, 14 * h:14 * h + 14], T.WSP[16 * h:16 * h + 1, 0:8 * C], [("WSP", 0, 8 * C)], [("MG", 14 * h, 14 * h + 14)]) for h in range(8)])
+        ts(("HB", 0, 14), ("I3", 16, 30), 1024.0, ("HADJ", 0, 1), ALU.mult, ALU.add)
+        ts(("HC", 0, 14), ("HB", 0, 14), 7168, None, ALU.bitwise_and)
+        ts(("HD", 0, 14), ("I3", 0, 14), 1, 1020, ALU.logical_shift_right, ALU.bitwise_and)
+        tt(("HO", 0, 14), ("HC", 0, 14), ("HD", 0, 14), ALU.add)
+        for t in range(4):
+            ts(("LH", 16 * t, 16 * t + 14), ("HO", 0, 14), float(t), None, ALU.add)
+        if last:
+            cp(("LB", 0, 14), ("I3", 0, 14))
+            op("v", lambda e: e.transpose(T.TR[:, 0:32], T.LB[:, 0:32]), [("LB", 0, 32)], [("TR", 0, 32)])
+        if rnd == 0:
+            quant("Vc", "Vp", 0, 128, "VIN", 0)
+        tt(("M1", 0, 56), ("MG", 0, 56), ("MG", 56, 112), ALU.add)
+        tt(("M2", 0, 28), ("M1", 0, 28), ("M1", 28, 56), ALU.add)
+        tt(("M3", 0, 14), ("M2", 0, 14), ("M2", 14, 28), ALU.add)
+        ts(("X1", 0, 14), ("M3", 0, 14), ("HADJ", 0, 1), None, ALU.add)
+        ts(("X2", 0, 14), ("X1", 0, 14), 8191, None, ALU.bitwise_and)
+        for t in (2, 0, 3, 1):
+            ts(("LF", 16 * t, 16 * t + 14), ("X2", 0, 14), float(t), None, ALU.add)
+        for t in (2, 0, 3, 1):
+            gather("vs"[t // 2], ("TL", t, 512, 4), ("WINF", 0, 8 * SLOT), ("LF", 16 * t, 16 * t + 8))
+        quant("Lc", "Lp", 0, 128, "TL", 0)
+        rid, pid = topo.addr(partners[rnd], core)
+        ls, ar = "ls%d" % rnd, "ar%d" % rnd
+        reads = spread([("Lc", 0, H), ("Lp", 0, H)])
+        before("g", "d", reads, [])
+        g.remote_dma(T[B + "c"][:, 128:240].bitcast(dt.uint8), T.Lc[:, 0:H].bitcast(dt.uint8), T.sem[ar], T.sem[ls], pid, rid, emask)
+        g.remote_dma(T[B + "p"][:, 128:240], T.Lp[:, 0:H], T.sem[ar], T.sem[ls], pid, rid, emask)
+        total[ls] = total[ar] = 2 * len(lanes)
+        after("g", "d", reads, [], ls, total[ls])
+        after("remote", "d", [], spread([(B + "c", 128, 240), (B + "p", 128, 240)]), ar, total[ar])
+        for t in (2, 0, 3, 1):
+            gather("vs"[t // 2], ("TU", t, 512, 4), ("WINF", 0, 8 * SLOT), ("LF", 16 * t + 6, 16 * t + 14))
+        quant(B + "c", B + "p", 0, 128, "TU", 0)
+        for r0, w0, w1 in ((0, 448, 896), (112, 0, 448)):
+            for b in range(4):
+                mm("PB%d" % b, "W", 128 * b, B, r0, 128)
+                op("s", lambda e: e.activation(T.RL[:, 128 * b:128 * b + H], T["PB%d" % b][:, 16:128], ACT.Relu, scale=0.03125), [("PB%d" % b, 0, 512)], [("RL", 128 * b, 128 * b + H)])
+                mm("PB%d" % (4 + b), "E", 128 * b, B, r0, 128)
+                tt(("WINT", w0 + b, w1, 4), ("PB%d" % (4 + b), 16, 128), ("RL", 128 * b, 128 * b + H), ALU.add)
+            replicate("WINT", w0, w1, "ys")
+        if last:
+            dmas([("ys"[h % 2], T.pl[h:h + 1, 0:C], T.TR[32 * (h // 2):32 * (h // 2) + 14, 16 * (h % 2):16 * (h % 2) + 16], [("TR", 0, 32)], []) for h in range(8)])
+        for t in (2, 0, 3, 1):
+            gather("vs"[t // 2], ("XT", t, 896, 4), ("WINT", 0, 8 * SLOT), ("LH", 16 * t, 16 * t + 14))
+        quant("Xc", "Xp", 0, C, "XT", 0)
+
+    mm("PB0", "V", 0, "X", 0, C)
+    acp(("Y", 0, C), ("PB0", 0, C))
+    dmas([("y", T.oc[:], T.Xc[:].bitcast(dt.uint8), [("Xc", 0, C)], [])]
+         + [("y", T.osc[4 * k:4 * k + 4, 0:C], T.Xp[32 * k:32 * k + 4, 0:C], [("Xp", 0, C)], []) for k in range(4)])
+    dmas([("s", T.y[:], T.Y[:, 0:C], [("Y", 0, C)], [])])
+    for sem, c in total.items():
+        learn("g", sem, c)

@@ -22,7 +22,7 @@ for _n, _w, _d in [
         ("XT", 4 * C, BF), ("UT", 512, BF), ("VIN", 512, BF), ("ET", 2048, BF), ("OT", 960, BF), ("WRT", 512, BF),
         ("SB", 8 * C, FP), ("SJ", 16, FP), ("R", 16, FP), ("J0", 8 * C, BF), ("J1", 8 * C, BF),
         ("WINF", 8 * SLOT, BF), ("WINT", 8 * SLOT, BF), ("WSP", 8 * C, FP), ("MG", 112, FP), ("M1", 56, FP), ("M2", 28, FP), ("M3", 14, FP),
-        ("X1", 16, I32), ("X2", 16, I32), ("LF", 64, U16), ("LH", 64, U16), ("SO", 16, U16),
+        ("X1", 16, I32), ("X2", 16, I32), ("LF", 16, U16), ("LH", 64, U16), ("SO", 16, U16),
         ("RI", 16, I32), ("D4", 64, I32), ("DB", 64, BF), ("RM", 512, BF), ("RB", 176, FP), ("RW", 16, FP),
         ("TM", C, FP), ("T1", 112, FP), ("T2", 56, FP), ("T3", 28, FP), ("T4", 14, FP), ("L1", 14, FP), ("LB", 32, FP), ("TR", 32, FP),
         ("I3", 48, I32), ("WP", 48, FP), ("PM", 48, FP), ("PA", 16, FP), ("PA2", 16, FP),
@@ -71,7 +71,7 @@ def rank_program(g, core, T, topo):
             out.append((r[0], 0, 512, None) if r[0][:2] == "PB" else (r + (None,))[:4])
         return out
 
-    def before(q, kind, reads, writes):
+    def before(q, reads, writes):
         need = {}
         for w, regs in ((False, reads), (True, writes)):
             for (b, lo, hi, ph) in regs:
@@ -91,9 +91,8 @@ def rank_program(g, core, T, topo):
     def after(q, kind, reads, writes, sem, c):
         for w, regs in ((False, reads), (True, writes)):
             for (b, lo, hi, ph) in regs:
-                old = hist.setdefault(b, [])
                 keep = []
-                for e in old:
+                for e in hist.get(b, []):
                     inside = e[0] >= lo and e[1] <= hi and (ph is None or ph == e[2])
                     if inside and ((w and b[:2] != "PB") or (e[4] == q and e[5] == "c" and kind == "c" and (e[3] == w or b[:2] == "PB"))):
                         if not (e[6] == sem and e[7] == c):
@@ -104,7 +103,7 @@ def rank_program(g, core, T, topo):
 
     def op(q, fn, reads, writes):
         reads, writes = spread(reads), spread(writes)
-        before(q, "c", reads, writes)
+        before(q, reads, writes)
         sem = SEM[q]
         fn(Q[q]).then_inc(T.sem[sem], 1)
         total[sem] = total.get(sem, 0) + 1
@@ -117,7 +116,7 @@ def rank_program(g, core, T, topo):
         sn = {}
         items = [(q, o, i, spread(r), spread(w)) for q, o, i, r, w in items]
         for q, o, i, r, w in items:
-            before(q, "d", r, w)
+            before(q, r, w)
             Q[q].dma_start(o, i).then_inc(T.sem[sem], 16)
             for s2, c2 in known[q].items():
                 sn[s2] = max(sn.get(s2, 0), c2)
@@ -140,14 +139,14 @@ def rank_program(g, core, T, topo):
     def rg(r):
         return (r[0], r[1], r[2], r[1] % 4) if len(r) > 3 and r[3] == 4 else (r[0], r[1], r[2])
 
-    def ts(out, in0, s1, s2, o0, o1=None, q="v"):
+    def ts(out, in0, s1, s2, o0, o1=None):
         rs = [rg(in0)] + [s for s in (s1, s2) if isinstance(s, tuple)]
         a1 = ap(s1) if isinstance(s1, tuple) else s1
         a2 = ap(s2) if isinstance(s2, tuple) else s2
         if o1 is None:
-            op(q, lambda e: e.tensor_scalar(ap(out), ap(in0), a1, None, o0), rs, [rg(out)])
+            op("v", lambda e: e.tensor_scalar(ap(out), ap(in0), a1, None, o0), rs, [rg(out)])
         else:
-            op(q, lambda e: e.tensor_scalar(ap(out), ap(in0), a1, a2, o0, o1), rs, [rg(out)])
+            op("v", lambda e: e.tensor_scalar(ap(out), ap(in0), a1, a2, o0, o1), rs, [rg(out)])
 
     def tt(out, a, b, o):
         op("v", lambda e: e.tensor_tensor(ap(out), ap(a), ap(b), o), [rg(a), rg(b)], [rg(out)])
@@ -179,33 +178,36 @@ def rank_program(g, core, T, topo):
     dmas([("y", T.Wc[:].bitcast(dt.uint8), T.wc[:], [], [("Wc", 0, 512)]), ("y", T.Wp[:], T.ws[:], [], [("Wp", 0, 512)]),
           ("y", T.VIN[:], T.v[:], [], [("VIN", 0, 512)])])
 
+    ms(("ET", 0, 2048), 1.0)
     iota(("UI", 0, 64), [[16, 8], [0, 8]], 0, 0)
     iota(("PI", 0, 8), [[0, 8]], 0, 1)
+    iota(("KI", 0, C), [[1, C]], 256, -1)
+    iota(("P8", 0, 8), [[-16, 8]], 0, 1)
+    op("g", lambda e: e.affine_select(T.ET[:], T.ET[:], [[1, 4], [-1, 512]], ALU.is_equal, 0.0, 0, 4), [("ET", 0, 2048)], [("ET", 0, 2048)])
+    iota(("IDV0", 0, C), [[1, C]], 0, 0, True)
+    iota(("NM0", 0, 14), [[16, 14]], 0, 1, True)
     cp(("UO", 0, 64), ("UI", 0, 64))
     ts(("JM", 0, 8), ("PI", 0, 8), 32, None, ALU.is_ge)
     ts(("JB", 0, 8), ("JM", 0, 8), -1.0, 1e29, ALU.add, ALU.mult)
-    ms(("ET", 0, 2048), 1.0)
-    op("g", lambda e: e.affine_select(T.ET[:], T.ET[:], [[1, 4], [-1, 512]], ALU.is_equal, 0.0, 0, 4), [("ET", 0, 2048)], [("ET", 0, 2048)])
-    iota(("KI", 0, C), [[1, C]], 256, -1)
-    iota(("P8", 0, 8), [[-16, 8]], 0, 1)
-    iota(("IDV0", 0, C), [[4, C]], 0, 0, True)
-    iota(("NM0", 0, 14), [[16, 14]], 0, 1, True)
-    for A in (1, 3, 2, 0):
-        ms(("VT%d" % A, 4 * (448 * A + 128), 4 * 448 * (A + 1)), 0.0)
+    ts(("KJ", 0, C), ("KI", 0, C), 15, None, ALU.bitwise_and)
+    ts(("DM", 0, C), ("KJ", 0, C), 0, None, ALU.is_equal)
+    for r, val in ((("OT", 0, 960), 0.0), (("RB", 128, 176), 0.0), (("D4", 0, 64), 0), (("I3", 0, 48), 0),
+                   (("WP", 0, 16), 1.75), (("WP", 16, 32), 222.25), (("WP", 32, 48), -223.0)):
+        ms(r, val)
+    ms(("OT", 448, 512), 1.0)
     quant("Uc", "Up", 0, 128, "UT", 0)
     op("s", lambda e: e.activation(T.UBp[:, 0:1024], T.Up[:, 0:128].indirect(T.UO[:, 0:64]), ACT.Copy),
        [("Up", 0, 128), ("UO", 0, 64)], [("UBp", 0, 1024)])
     op("v", lambda e: e.tensor_copy(T.UBc[:, 0:1024].bitcast(dt.uint32), T.Uc[:, 0:128].bitcast(dt.uint32).indirect(T.UO[:, 0:64])),
        [("Uc", 0, 128), ("UO", 0, 64)], [("UBc", 0, 1024)])
     quant("Xc", "Xp", 0, C, "XT", 0)
-    quant("Ec", "Ep", 0, 512, "ET", 0)
+
+    def zeros():
+        for A in range(4):
+            ms(("VT%d" % A, 4 * (448 * A + 128), 4 * 448 * (A + 1)), 0.0)
 
     def more_constants():
-        ms(("OT", 0, 960), 0.0)
-        ms(("OT", 448, 512), 1.0)
         quant("Oc", "Op", 0, 240, "OT", 0)
-        ts(("KJ", 0, C), ("KI", 0, C), 15, None, ALU.bitwise_and)
-        ts(("DM", 0, C), ("KJ", 0, C), 0, None, ALU.is_equal)
         ms(("WRT", 0, 512), 0.0)
         for d, w in enumerate((1.0, 16.0, 256.0)):
             ts(("WRT", d, 512, 4), ("DM", 0, 128), w, None, ALU.mult)
@@ -225,15 +227,6 @@ def rank_program(g, core, T, topo):
         tt(("CD", 0, 8), ("CA", 0, 8), ("CB", 0, 8), ALU.add)
         tt(("CE", 0, 8), ("CC", 0, 8), ("CD", 0, 8), ALU.add)
         cp(("CGO", 0, 8), ("CE", 0, 8))
-        ms(("RB", 0, 176), 0.0)
-        ms(("D4", 0, 64), 0)
-        ms(("LB", 0, 32), 0.0)
-        ms(("I3", 0, 48), 0)
-        for k, w in enumerate((1.75, 222.25, -223.0)):
-            ms(("WP", 16 * k, 16 * k + 16), w)
-        for k in range(8):
-            ms(("WINF", SLOT * k + 896, SLOT * k + SLOT), 0.0)
-            ms(("WINT", SLOT * k + 896, SLOT * k + SLOT), 0.0)
 
     def replicate(win, lo, hi, queues):
         items = []
@@ -259,12 +252,12 @@ def rank_program(g, core, T, topo):
         for h in range(8):
             mm("PB%d" % (h % 4), "UB", 128 * h, "X", 0, C)
             (cp if h in (1, 3) else acp)(("SB", C * h, C * h + C), ("PB%d" % (h % 4), 0, C))
+        if rnd == 0:
+            quant("Ec", "Ep", 0, 512, "ET", 0)
         for b in range(4):
             mm("PB%d" % b, "E", 128 * b, "X", 0, C)
-            acp(("WINF", b, 896, 4), ("PB%d" % b, 0, C))
+            acp(("WINF", C * b, C * b + C), ("PB%d" % b, 0, C))
         replicate("WINF", 0, 896, "y")
-
-        first = [True]
 
         def compare(a):
             A, t, h, half = a // 4, a % 4, a // 2, a % 2
@@ -278,39 +271,37 @@ def rank_program(g, core, T, topo):
             op("s", lambda e: e.activation(T[j][:, 0:n], T[vt][:, t:4 * n:4], ACT.Copy, accum_out=T.R[:, a:a + 1]),
                [(vt, t, 4 * n, t)], [(j, 0, n), ("R", a, a + 1)])
 
-        def count(A, final):
-            for p in range(A + 1):
-                quant("K%dc" % A, "K%dp" % A, 448 * p, 448, "VT%d" % A, 1792 * p)
-                for h in (2 * p, 2 * p + 1):
-                    mm("PB6", "O", 112 - 16 * h, "K%d" % A, C * h, C, first[0], final and h == 2 * A + 1)
-                    first[0] = False
+        def count(A, p, first=False, final=False):
+            quant("K%dc" % A, "K%dp" % A, 448 * p, 448, "VT%d" % A, 1792 * p)
+            for h in (2 * p, 2 * p + 1):
+                mm("PB6", "O", 112 - 16 * h, "K%d" % A, C * h, C, first and h == 2 * p, final and h == 2 * p + 1)
 
-        for a in (4, 5, 6, 7):
+        for a in (4, 5, 6, 7, 12, 13, 14, 15, 8, 9, 10, 11, 0, 1, 2, 3):
             compare(a)
+            if rnd == 0 and a == 4:
+                zeros()
         iota(("WSP", 0, 8 * C), [[0, 8 * C]], 0, 0, True)
-        for a in (12, 13):
-            compare(a)
         if rnd == 0:
             more_constants()
-        count(1, False)
-        for a in (14, 15, 8, 9):
-            compare(a)
-        count(3, False)
-        for a in (10, 11, 0, 1, 2, 3):
-            compare(a)
-        count(2, False)
-        count(0, True)
+        count(1, 0, True)
+        count(1, 1)
+        for p in range(4):
+            count(3, p)
+        count(2, 0)
         cp(("RI", 0, 16), ("R", 0, 16))
+        count(2, 1)
         ts(("D4", 0, 64, 4), ("RI", 0, 16), 15, None, ALU.bitwise_and)
         ts(("D4", 1, 64, 4), ("RI", 0, 16), 4, 15, ALU.logical_shift_right, ALU.bitwise_and)
         ts(("D4", 2, 64, 4), ("RI", 0, 16), 8, None, ALU.logical_shift_right)
         cp(("DB", 0, 64), ("D4", 0, 64))
+        count(2, 2)
         for k in range(8):
             o = ("RM", 64 * k, 64 * k + 64)
-            if k % 2:
+            if k % 4:
                 op("s", lambda e: e.activation(ap(o), T.DB[:, 0:64], ACT.Copy, scale=T.MK[:, k:k + 1]), [("DB", 0, 64), ("MK", k, k + 1)], [rg(o)])
             else:
                 ts(o, ("DB", 0, 64), ("MK", k, k + 1), None, ALU.mult)
+        count(0, 0, False, True)
         quant("RQc", "RQp", 0, 128, "RM", 0)
         mm("PB7", "WR", 0, "RQ", 0, 128)
         acp(("RB", 0, 128), ("PB7", 0, 128))
@@ -320,8 +311,10 @@ def rank_program(g, core, T, topo):
             w = src[1]
             tt((nxt, 0, w // 2), (src[0], 0, w, 2), (src[0], 1, w, 2), ALU.add)
             src = (nxt, w // 2)
-        gather("v", ("RW", 0, 16), ("RB", 0, 176), ("CGO", 0, 1))
-        tt(("L1", 0, 14), ("NM", 0, 14), ("RW", 0, 14), ALU.subtract)
+            if nxt == "T2":
+                gather("v", ("RW", 0, 16), ("RB", 0, 176), ("CGO", 0, 1))
+            if nxt == "T3":
+                tt(("L1", 0, 14), ("NM", 0, 14), ("RW", 0, 14), ALU.subtract)
         tt(("I3", 0, 14), ("L1", 0, 14), ("T4", 0, 14), ALU.add)
         ts(("I3", 16, 30), ("I3", 0, 14), 7, None, ALU.bitwise_and)
         ts(("I3", 32, 46), ("I3", 0, 14), 7, None, ALU.logical_shift_right)
@@ -339,31 +332,34 @@ def rank_program(g, core, T, topo):
         for t in range(4):
             ts(("LH", 16 * t, 16 * t + 14), ("HO", 0, 14), float(t), None, ALU.add)
         if last:
+            ms(("LB", 0, 32), 0.0)
             cp(("LB", 0, 14), ("I3", 0, 14))
             op("v", lambda e: e.transpose(T.TR[:, 0:32], T.LB[:, 0:32]), [("LB", 0, 32)], [("TR", 0, 32)])
         if rnd == 0:
             quant("Vc", "Vp", 0, 128, "VIN", 0)
+            for k in range(8):
+                ms(("WINF", SLOT * k + 896, SLOT * k + SLOT), 0.0)
+                ms(("WINT", SLOT * k + 896, SLOT * k + SLOT), 0.0)
         tt(("M1", 0, 56), ("MG", 0, 56), ("MG", 56, 112), ALU.add)
         tt(("M2", 0, 28), ("M1", 0, 28), ("M1", 28, 56), ALU.add)
         tt(("M3", 0, 14), ("M2", 0, 14), ("M2", 14, 28), ALU.add)
         ts(("X1", 0, 14), ("M3", 0, 14), ("HADJ", 0, 1), None, ALU.add)
         ts(("X2", 0, 14), ("X1", 0, 14), 8191, None, ALU.bitwise_and)
+        cp(("LF", 0, 14), ("X2", 0, 14))
         for t in (2, 0, 3, 1):
-            ts(("LF", 16 * t, 16 * t + 14), ("X2", 0, 14), float(t), None, ALU.add)
-        for t in (2, 0, 3, 1):
-            gather("vs"[t // 2], ("TL", t, 512, 4), ("WINF", 0, 8 * SLOT), ("LF", 16 * t, 16 * t + 8))
+            gather("vs"[t // 2], ("TL", t, 512, 4), ("WINF", C * t, 8 * SLOT), ("LF", 0, 8))
         quant("Lc", "Lp", 0, 128, "TL", 0)
         rid, pid = topo.addr(partners[rnd], core)
         ls, ar = "ls%d" % rnd, "ar%d" % rnd
         reads = spread([("Lc", 0, H), ("Lp", 0, H)])
-        before("g", "d", reads, [])
+        before("g", reads, [])
         g.remote_dma(T[B + "c"][:, 128:240].bitcast(dt.uint8), T.Lc[:, 0:H].bitcast(dt.uint8), T.sem[ar], T.sem[ls], pid, rid, emask)
         g.remote_dma(T[B + "p"][:, 128:240], T.Lp[:, 0:H], T.sem[ar], T.sem[ls], pid, rid, emask)
         total[ls] = total[ar] = 2 * len(lanes)
         after("g", "d", reads, [], ls, total[ls])
         after("remote", "d", [], spread([(B + "c", 128, 240), (B + "p", 128, 240)]), ar, total[ar])
         for t in (2, 0, 3, 1):
-            gather("vs"[t // 2], ("TU", t, 512, 4), ("WINF", 0, 8 * SLOT), ("LF", 16 * t + 6, 16 * t + 14))
+            gather("vs"[t // 2], ("TU", t, 512, 4), ("WINF", C * t, 8 * SLOT), ("LF", 6, 14))
         quant(B + "c", B + "p", 0, 128, "TU", 0)
         for r0, w0, w1 in ((0, 448, 896), (112, 0, 448)):
             for b in range(4):

from concourse.bass import DstId, RemoteDMATransfer
from concourse.mybir import dt, AluOpType as ALU, ActivationFunctionType as ACT

C, H = 224, 112
MASK = [1, 2, 4]
SLOT = 1024
F8, U8, BF, FP, I32, U16 = "float8_e4m3fn_x4", "uint8", "bfloat16", "float32", "int32", "uint16"

SCRATCH = {}


def _sb(name, n, d):
    SCRATCH[name] = ("sbuf", [128, n], d)


def _mx(code, plane, n):
    _sb(code, n, F8)
    _sb(plane, n, U8)


for _n, _w, _d in [
        ("XT", 4 * C, BF), ("UT", 512, BF), ("VIN", 512, BF), ("ET", 2048, BF), ("OT", 960, BF), ("WRT", 512, BF),
        ("SB", 8 * C, FP), ("SJ", 16, FP), ("R", 16, FP), ("J0", 8 * C, BF), ("J1", 8 * C, BF),
        ("WINF", 8 * SLOT, BF), ("WINT", 8 * SLOT, BF), ("WSP", 8 * C, FP), ("MG", 112, FP), ("M1", 56, FP), ("M2", 28, FP), ("M3", 14, FP),
        ("X1", 16, I32), ("X2", 16, I32), ("LF", 16, U16), ("LH", 64, U16), ("SO", 16, U16),
        ("RI", 16, I32), ("D4", 64, I32), ("DB", 64, BF), ("RM", 512, BF), ("RB", 176, FP), ("RW", 16, FP),
        ("TM", C, FP), ("T1", 112, FP), ("T2", 56, FP), ("T3", 28, FP), ("T4", 14, FP), ("L1", 14, FP), ("LB", 32, FP), ("TR", 32, FP),
        ("I3", 48, I32), ("WP", 48, FP), ("PM", 48, FP), ("PA", 16, FP), ("PA2", 16, FP),
        ("HB", 16, I32), ("HC", 16, I32), ("HD", 16, I32), ("HO", 16, I32),
        ("TL", 512, BF), ("TU", 512, BF), ("RL", 512, FP), ("Y", C, FP),
        ("KI", C, I32), ("KJ", C, I32), ("DM", C, FP), ("P8", 8, I32), ("P9", 8, I32), ("MK", 8, FP), ("PI", 8, I32), ("GI", 8, I32), ("EI", 8, I32),
        ("HADJ", 8, FP), ("G1024", 8, FP), ("IDV0", C, FP), ("IDV", C, FP), ("NM0", 14, FP), ("G208", 8, FP), ("NM", 14, FP),
        ("CA", 8, FP), ("CB", 8, FP), ("CC", 8, FP), ("CD", 8, FP), ("CE", 8, FP), ("CGO", 8, U16), ("UI", 64, I32), ("UO", 64, U16), ("JM", 8, FP), ("JB", 8, FP)]:
    _sb(_n, _w, _d)
for _n, _w in [("X", C), ("U", 128), ("UB", 1024), ("V", 128), ("W", 512), ("E", 512), ("O", 240), ("WR", 128), ("RQ", 128), ("L", 128), ("B0", 240), ("B1", 240), ("B2", 240)]:
    _mx(_n + "c", _n + "p", _w)
for _a in range(4):
    _sb("VT%d" % _a, 4 * 448 * (_a + 1), BF)
    _mx("K%dc" % _a, "K%dp" % _a, 448 * (_a + 1))
for _n in range(8):
    SCRATCH["PB%d" % _n] = ("psum", [128, 512], FP)

SEMAPHORES = ["cv", "cs", "ct", "cg"] + ["d%d" % k for k in range(60)] + ["ls%d" % k for k in range(3)] + ["ar%d" % k for k in range(3)]


def rank_program(g, core, T, topo):
    rank = T.rank_of(core)
    if rank is None:
        return
    Q = {"v": g.vector, "s": g.scalar, "t": g.tensor, "g": g, "y": g.sync}
    SEM = {"v": "cv", "s": "cs", "t": "ct", "g": "cg"}
    total = {}
    known = {q: {} for q in Q}
    snap = {}
    hist = {}
    nd = [0]

    def learn(q, sem, c):
        k = known[q]
        if k.get(sem, 0) >= c:
            return
        Q[q].wait_ge(T.sem[sem], c)
        k[sem] = c
        for s2, c2 in snap.get((sem, c), {}).items():
            if k.get(s2, 0) < c2:
                k[s2] = c2

    def spread(regs):
        out = []
        for r in regs:
            out.append((r[0], 0, 512, None) if r[0][:2] == "PB" else (r + (None,))[:4])
        return out

    def before(q, reads, writes):
        need = {}
        for w, regs in ((False, reads), (True, writes)):
            for (b, lo, hi, ph) in regs:
                for e in hist.get(b, []):
                    elo, ehi, eph, ew, eq, ek, es, ec = e
                    if elo >= hi or lo >= ehi or (ph is not None and eph is not None and ph != eph):
                        continue
                    if b[:2] == "PB":
                        if eq == q:
                            continue
                    elif not (w or ew):
                        continue
                    need[es] = max(need.get(es, 0), ec)
        for s, c in sorted(need.items(), key=lambda x: -len(snap.get(x, {}))):
            learn(q, s, c)

    def after(q, kind, reads, writes, sem, c):
        for w, regs in ((False, reads), (True, writes)):
            for (b, lo, hi, ph) in regs:
                keep = []
                for e in hist.get(b, []):
                    inside = e[0] >= lo and e[1] <= hi and (ph is None or ph == e[2])
                    if inside and ((w and b[:2] != "PB") or (e[4] == q and e[5] == "c" and kind == "c" and (e[3] == w or b[:2] == "PB"))):
                        if not (e[6] == sem and e[7] == c):
                            continue
                    keep.append(e)
                keep.append((lo, hi, ph, w, q, kind, sem, c))
                hist[b] = keep

    def op(q, fn, reads, writes):
        reads, writes = spread(reads), spread(writes)
        before(q, reads, writes)
        sem = SEM[q]
        fn(Q[q]).then_inc(T.sem[sem], 1)
        total[sem] = total.get(sem, 0) + 1
        snap[(sem, total[sem])] = dict(known[q])
        after(q, "c", reads, writes, sem, total[sem])

    def dmas(items):
        sem = "d%d" % nd[0]
        nd[0] += 1
        sn = {}
        items = [(q, o, i, spread(r), spread(w)) for q, o, i, r, w in items]
        for q, o, i, r, w in items:
            before(q, r, w)
            Q[q].dma_start(o, i).then_inc(T.sem[sem], 16)
            for s2, c2 in known[q].items():
                sn[s2] = max(sn.get(s2, 0), c2)
        total[sem] = 16 * len(items)
        snap[(sem, total[sem])] = sn
        for q, o, i, r, w in items:
            after(q, "d", r, w, sem, total[sem])

    def quant(code, plane, a, n, src, s0):
        op("v", lambda e: e.quantize_mx(T[code][:, a:a + n], T[plane][:, a:a + n], T[src][:, s0:s0 + 4 * n]),
           [(src, s0, s0 + 4 * n)], [(code, a, a + n), (plane, a, a + n)])

    def mm(bank, L, l0, R, r0, n, start=True, stop=True):
        op("t", lambda e: e.matmul_mx(T[bank][:, 0:n], T[L + "c"][:, l0:l0 + 128], T[L + "p"][:, l0:l0 + 128], T[R + "c"][:, r0:r0 + n], T[R + "p"][:, r0:r0 + n], start, stop),
           [(L + "c", l0, l0 + 128), (L + "p", l0, l0 + 128), (R + "c", r0, r0 + n), (R + "p", r0, r0 + n)], [(bank, 0, 512)])

    def ap(r):
        return T[r[0]][:, r[1]:r[2]:r[3]] if len(r) > 3 else T[r[0]][:, r[1]:r[2]]

    def rg(r):
        return (r[0], r[1], r[2], r[1] % 4) if len(r) > 3 and r[3] == 4 else (r[0], r[1], r[2])

    def ts(out, in0, s1, s2, o0, o1=None):
        rs = [rg(in0)] + [s for s in (s1, s2) if isinstance(s, tuple)]
        a1 = ap(s1) if isinstance(s1, tuple) else s1
        a2 = ap(s2) if isinstance(s2, tuple) else s2
        if o1 is None:
            op("v", lambda e: e.tensor_scalar(ap(out), ap(in0), a1, None, o0), rs, [rg(out)])
        else:
            op("v", lambda e: e.tensor_scalar(ap(out), ap(in0), a1, a2, o0, o1), rs, [rg(out)])

    def tt(out, a, b, o):
        op("v", lambda e: e.tensor_tensor(ap(out), ap(a), ap(b), o), [rg(a), rg(b)], [rg(out)])

    def cp(out, a):
        op("v", lambda e: e.tensor_copy(ap(out), ap(a)), [rg(a)], [rg(out)])

    def acp(out, a):
        op("s", lambda e: e.activation(ap(out), ap(a), ACT.Copy), [rg(a)], [rg(out)])

    def ms(out, val):
        op("v", lambda e: e.memset(ap(out), val), [], [rg(out)])

    def iota(out, pattern, base, mult, flag=False):
        if flag:
            op("g", lambda e: e.iota(ap(out), pattern, base, mult, allow_small_or_imprecise_dtypes=True), [], [rg(out)])
        else:
            op("g", lambda e: e.iota(ap(out), pattern, base, mult), [], [rg(out)])

    def gather(q, out, win, off):
        src = ap(win).indirect(ap(off))
        if q == "v":
            op("v", lambda e: e.tensor_copy(ap(out), src), [rg(win), rg(off)], [rg(out)])
        else:
            op("s", lambda e: e.activation(ap(out), src, ACT.Copy), [rg(win), rg(off)], [rg(out)])

    dmas([("y", T.XT[:], T.x[:], [], [("XT", 0, 4 * C)])])
    dmas([("s", T.UT[:], T.u[:], [], [("UT", 0, 512)])])
    dmas([("y", T.Wc[:].bitcast(dt.uint8), T.wc[:], [], [("Wc", 0, 512)]), ("y", T.Wp[:], T.ws[:], [], [("Wp", 0, 512)]),
          ("y", T.VIN[:], T.v[:], [], [("VIN", 0, 512)])])

    ms(("ET", 0, 2048), 1.0)
    iota(("UI", 0, 64), [[16, 8], [0, 8]], 0, 0)
    iota(("PI", 0, 8), [[0, 8]], 0, 1)
    iota(("KI", 0, C), [[1, C]], 256, -1)
    iota(("P8", 0, 8), [[-16, 8]], 0, 1)
    op("g", lambda e: e.affine_select(T.ET[:], T.ET[:], [[1, 4], [-1, 512]], ALU.is_equal, 0.0, 0, 4), [("ET", 0, 2048)], [("ET", 0, 2048)])
    iota(("IDV0", 0, C), [[1, C]], 0, 0, True)
    iota(("NM0", 0, 14), [[16, 14]], 0, 1, True)
    cp(("UO", 0, 64), ("UI", 0, 64))
    ts(("JM", 0, 8), ("PI", 0, 8), 32, None, ALU.is_ge)
    ts(("JB", 0, 8), ("JM", 0, 8), -1.0, 1e29, ALU.add, ALU.mult)
    ts(("KJ", 0, C), ("KI", 0, C), 15, None, ALU.bitwise_and)
    ts(("DM", 0, C), ("KJ", 0, C), 0, None, ALU.is_equal)
    for r, val in ((("OT", 0, 960), 0.0), (("RB", 128, 176), 0.0), (("D4", 0, 64), 0), (("I3", 0, 48), 0),
                   (("WP", 0, 16), 1.75), (("WP", 16, 32), 222.25), (("WP", 32, 48), -223.0)):
        ms(r, val)
    ms(("OT", 448, 512), 1.0)
    quant("Uc", "Up", 0, 128, "UT", 0)
    op("s", lambda e: e.activation(T.UBp[:, 0:1024], T.Up[:, 0:128].indirect(T.UO[:, 0:64]), ACT.Copy),
       [("Up", 0, 128), ("UO", 0, 64)], [("UBp", 0, 1024)])
    op("v", lambda e: e.tensor_copy(T.UBc[:, 0:1024].bitcast(dt.uint32), T.Uc[:, 0:128].bitcast(dt.uint32).indirect(T.UO[:, 0:64])),
       [("Uc", 0, 128), ("UO", 0, 64)], [("UBc", 0, 1024)])
    quant("Xc", "Xp", 0, C, "XT", 0)

    def zeros():
        for A in range(4):
            ms(("VT%d" % A, 4 * (448 * A + 128), 4 * 448 * (A + 1)), 0.0)

    def more_constants():
        quant("Oc", "Op", 0, 240, "OT", 0)
        ms(("WRT", 0, 512), 0.0)
        for d, w in enumerate((1.0, 16.0, 256.0)):
            ts(("WRT", d, 512, 4), ("DM", 0, 128), w, None, ALU.mult)
        quant("WRc", "WRp", 0, 128, "WRT", 0)
        ts(("P9", 0, 8), ("P8", 0, 8), 4, None, ALU.arith_shift_right)
        ts(("MK", 0, 8), ("P9", 0, 8), 0, None, ALU.is_equal)
        ts(("GI", 0, 8), ("PI", 0, 8), 4, None, ALU.arith_shift_right)
        ts(("EI", 0, 8), ("PI", 0, 8), 15, None, ALU.bitwise_and)
        ts(("HADJ", 0, 8), ("GI", 0, 8), -1024.0, 8192.0, ALU.mult, ALU.add)
        ts(("G1024", 0, 8), ("GI", 0, 8), 1024.0, None, ALU.mult)
        ts(("G208", 0, 8), ("GI", 0, 8), 208.0, None, ALU.mult)
        ts(("IDV", 0, C), ("IDV0", 0, C), ("G1024", 0, 1), None, ALU.add)
        ts(("NM", 0, 14), ("NM0", 0, 14), ("G208", 0, 1), None, ALU.add)
        ts(("CA", 0, 8), ("EI", 0, 8), 8, -95.0, ALU.is_ge, ALU.mult)
        ts(("CB", 0, 8), ("EI", 0, 8), 16.0, None, ALU.mult)
        ts(("CC", 0, 8), ("GI", 0, 8), 2.0, None, ALU.mult)
        tt(("CD", 0, 8), ("CA", 0, 8), ("CB", 0, 8), ALU.add)
        tt(("CE", 0, 8), ("CC", 0, 8), ("CD", 0, 8), ALU.add)
        cp(("CGO", 0, 8), ("CE", 0, 8))

    def replicate(win, lo, hi, queues):
        items = []
        for k in range(1, 8):
            o = SLOT * k
            p = 128 - 16 * k
            rd, wr = [(win, lo, hi)], [(win, o + lo, o + hi)]
            items.append((queues[k % len(queues)], T[win][0:p, o + lo:o + hi], T[win][16 * k:128, lo:hi], rd, wr))
            items.append((queues[(k + 1) % len(queues)], T[win][p:128, o + lo:o + hi], T[win][0:16 * k, lo:hi], rd, wr))
        dmas(items)

    partners = [T.cores[rank ^ m] for m in MASK]
    lanes = [e for e in topo.engines(core, partners[0]) if all(e in topo.engines(core, p) for p in partners)]
    emask = sum(1 << e for e in lanes)

    for rnd in range(3):
        B = "B%d" % rnd
        last = rnd == 2
        for half in range(2):
            mm("PB%d" % (4 + half), "X", 96 * half, "U", 0, 128)
        cp(("SJ", 0, 16, 2), ("PB4", 0, 128, 16))
        ts(("SJ", 1, 16, 2), ("PB5", 0, 128, 16), ("JM", 0, 1), ("JB", 0, 1), ALU.mult, ALU.add)
        for h in range(8):
            mm("PB%d" % (h % 4), "UB", 128 * h, "X", 0, C)
            (cp if h in (1, 3) else acp)(("SB", C * h, C * h + C), ("PB%d" % (h % 4), 0, C))
        if rnd == 0:
            quant("Ec", "Ep", 0, 512, "ET", 0)
        for b in range(4):
            mm("PB%d" % b, "E", 128 * b, "X", 0, C)
            acp(("WINF", C * b, C * b + C), ("PB%d" % b, 0, C))
        replicate("WINF", 0, 896, "y")

        def compare(a):
            A, t, h, half = a // 4, a % 4, a // 2, a % 2
            n = C * h + (C if half else 128)
            i0, m = (C * h + 128, 96) if half else (C * h, 128)
            vt = "VT%d" % A
            ts((vt, t, 4 * n, 4), ("SB", 0, n), ("SJ", a, a + 1), None, ALU.is_lt)
            d = (vt, 4 * i0 + t, 4 * n, 4)
            op("g", lambda e: e.affine_select(ap(d), ap(d), [[-1, m]], ALU.is_gt, 0.0, -32 * half, 1), [rg(d)], [rg(d)])
            j = "J%d" % (a % 2)
            op("s", lambda e: e.activation(T[j][:, 0:n], T[vt][:, t:4 * n:4], ACT.Copy, accum_out=T.R[:, a:a + 1]),
               [(vt, t, 4 * n, t)], [(j, 0, n), ("R", a, a + 1)])

        def count(A, p, first=False, final=False):
            quant("K%dc" % A, "K%dp" % A, 448 * p, 448, "VT%d" % A, 1792 * p)
            for h in (2 * p, 2 * p + 1):
                mm("PB6", "O", 112 - 16 * h, "K%d" % A, C * h, C, first and h == 2 * p, final and h == 2 * p + 1)

        for a in (4, 5, 6, 7, 12, 13, 14, 15, 8, 9, 10, 11, 0, 1, 2, 3):
            compare(a)
            if rnd == 0 and a == 4:
                zeros()
        iota(("WSP", 0, 8 * C), [[0, 8 * C]], 0, 0, True)
        if rnd == 0:
            more_constants()
        count(1, 0, True)
        count(1, 1)
        for p in range(4):
            count(3, p)
        count(2, 0)
        cp(("RI", 0, 16), ("R", 0, 16))
        count(2, 1)
        ts(("D4", 0, 64, 4), ("RI", 0, 16), 15, None, ALU.bitwise_and)
        ts(("D4", 1, 64, 4), ("RI", 0, 16), 4, 15, ALU.logical_shift_right, ALU.bitwise_and)
        ts(("D4", 2, 64, 4), ("RI", 0, 16), 8, None, ALU.logical_shift_right)
        cp(("DB", 0, 64), ("D4", 0, 64))
        count(2, 2)
        for k in range(8):
            o = ("RM", 64 * k, 64 * k + 64)
            if k % 4:
                op("s", lambda e: e.activation(ap(o), T.DB[:, 0:64], ACT.Copy, scale=T.MK[:, k:k + 1]), [("DB", 0, 64), ("MK", k, k + 1)], [rg(o)])
            else:
                ts(o, ("DB", 0, 64), ("MK", k, k + 1), None, ALU.mult)
        count(0, 0, False, True)
        quant("RQc", "RQp", 0, 128, "RM", 0)
        mm("PB7", "WR", 0, "RQ", 0, 128)
        acp(("RB", 0, 128), ("PB7", 0, 128))
        tt(("TM", 0, C), ("PB6", 0, C), ("DM", 0, C), ALU.mult)
        src = ("TM", C)
        for nxt in ("T1", "T2", "T3", "T4"):
            w = src[1]
            tt((nxt, 0, w // 2), (src[0], 0, w, 2), (src[0], 1, w, 2), ALU.add)
            src = (nxt, w // 2)
            if nxt == "T2":
                gather("v", ("RW", 0, 16), ("RB", 0, 176), ("CGO", 0, 1))
            if nxt == "T3":
                tt(("L1", 0, 14), ("NM", 0, 14), ("RW", 0, 14), ALU.subtract)
        tt(("I3", 0, 14), ("L1", 0, 14), ("T4", 0, 14), ALU.add)
        ts(("I3", 16, 30), ("I3", 0, 14), 7, None, ALU.bitwise_and)
        ts(("I3", 32, 46), ("I3", 0, 14), 7, None, ALU.logical_shift_right)
        tt(("PM", 0, 48), ("I3", 0, 48), ("WP", 0, 48), ALU.mult)
        tt(("PA", 0, 16), ("PM", 0, 16), ("PM", 16, 32), ALU.add)
        tt(("PA2", 0, 16), ("PA", 0, 16), ("PM", 32, 48), ALU.add)
        cp(("SO", 0, 16), ("PA2", 0, 16))
        op("v", lambda e: e.tensor_copy(T.WSP[:, 0:8 * C].indirect(T.SO[:, 0:14]), T.IDV[:, 0:C]),
           [("SO", 0, 14), ("IDV", 0, C)], [("WSP", 0, 8 * C)])
        dmas([("ys"[h % 2], T.MG[:, 14 * h:14 * h + 14], T.WSP[16 * h:16 * h + 1, 0:8 * C], [("WSP", 0, 8 * C)], [("MG", 14 * h, 14 * h + 14)]) for h in range(8)])
        ts(("HB", 0, 14), ("I3", 16, 30), 1024.0, ("HADJ", 0, 1), ALU.mult, ALU.add)
        ts(("HC", 0, 14), ("HB", 0, 14), 7168, None, ALU.bitwise_and)
        ts(("HD", 0, 14), ("I3", 0, 14), 1, 1020, ALU.logical_shift_right, ALU.bitwise_and)
        tt(("HO", 0, 14), ("HC", 0, 14), ("HD", 0, 14), ALU.add)
        for t in range(4):
            ts(("LH", 16 * t, 16 * t + 14), ("HO", 0, 14), float(t), None, ALU.add)
        if last:
            ms(("LB", 0, 32), 0.0)
            cp(("LB", 0, 14), ("I3", 0, 14))
            op("v", lambda e: e.transpose(T.TR[:, 0:32], T.LB[:, 0:32]), [("LB", 0, 32)], [("TR", 0, 32)])
        if rnd == 0:
            quant("Vc", "Vp", 0, 128, "VIN", 0)
            for k in range(8):
                ms(("WINF", SLOT * k + 896, SLOT * k + SLOT), 0.0)
                ms(("WINT", SLOT * k + 896, SLOT * k + SLOT), 0.0)
        tt(("M1", 0, 56), ("MG", 0, 56), ("MG", 56, 112), ALU.add)
        tt(("M2", 0, 28), ("M1", 0, 28), ("M1", 28, 56), ALU.add)
        tt(("M3", 0, 14), ("M2", 0, 14), ("M2", 14, 28), ALU.add)
        ts(("X1", 0, 14), ("M3", 0, 14), ("HADJ", 0, 1), None, ALU.add)
        ts(("X2", 0, 14), ("X1", 0, 14), 8191, None, ALU.bitwise_and)
        cp(("LF", 0, 14), ("X2", 0, 14))
        for t in (2, 0, 3, 1):
            gather("vs"[t // 2], ("TL", t, 512, 4), ("WINF", C * t, 8 * SLOT), ("LF", 0, 8))
        quant("Lc", "Lp", 0, 128, "TL", 0)
        rid, pid = topo.addr(partners[rnd], core)
        ls, ar = "ls%d" % rnd, "ar%d" % rnd
        reads = spread([("Lc", 0, H), ("Lp", 0, H)])
        before("g", reads, [])
        g.remote_dma(T[B + "c"][:, 128:240].bitcast(dt.uint8), T.Lc[:, 0:H].bitcast(dt.uint8), T.sem[ar], T.sem[ls], pid, rid, emask)
        g.remote_dma(T[B + "p"][:, 128:240], T.Lp[:, 0:H], T.sem[ar], T.sem[ls], pid, rid, emask)
        total[ls] = total[ar] = 2 * len(lanes)
        after("g", "d", reads, [], ls, total[ls])
        after("remote", "d", [], spread([(B + "c", 128, 240), (B + "p", 128, 240)]), ar, total[ar])
        for t in (2, 0, 3, 1):
            gather("vs"[t // 2], ("TU", t, 512, 4), ("WINF", C * t, 8 * SLOT), ("LF", 6, 14))
        quant(B + "c", B + "p", 0, 128, "TU", 0)
        for r0, w0, w1 in ((0, 448, 896), (112, 0, 448)):
            for b in range(4):
                mm("PB%d" % b, "W", 128 * b, B, r0, 128)
                op("s", lambda e: e.activation(T.RL[:, 128 * b:128 * b + H], T["PB%d" % b][:, 16:128], ACT.Relu, scale=0.03125), [("PB%d" % b, 0, 512)], [("RL", 128 * b, 128 * b + H)])
                mm("PB%d" % (4 + b), "E", 128 * b, B, r0, 128)
                tt(("WINT", w0 + b, w1, 4), ("PB%d" % (4 + b), 16, 128), ("RL", 128 * b, 128 * b + H), ALU.add)
            replicate("WINT", w0, w1, "ys")
        if last:
            dmas([("ys"[h % 2], T.pl[h:h + 1, 0:C], T.TR[32 * (h // 2):32 * (h // 2) + 14, 16 * (h % 2):16 * (h % 2) + 16], [("TR", 0, 32)], []) for h in range(8)])
        for t in (2, 0, 3, 1):
            gather("vs"[t // 2], ("XT", t, 896, 4), ("WINT", 0, 8 * SLOT), ("LH", 16 * t, 16 * t + 14))
        quant("Xc", "Xp", 0, C, "XT", 0)

    mm("PB0", "V", 0, "X", 0, C)
    acp(("Y", 0, C), ("PB0", 0, C))
    dmas([("y", T.oc[:], T.Xc[:].bitcast(dt.uint8), [("Xc", 0, C)], [])]
         + [("y", T.osc[4 * k:4 * k + 4, 0:C], T.Xp[32 * k:32 * k + 4, 0:C], [("Xp", 0, C)], []) for k in range(4)])
    dmas([("s", T.y[:], T.Y[:, 0:C], [("Y", 0, C)], [])])
    for sem, c in total.items():
        learn("g", sem, c)
